import numpy as np
import ml_dtypes


def mxq(x, axis, fmt="e4m3"):
    dtype, down = {"e4m3": (ml_dtypes.float8_e4m3fn, 7), "e5m2": (ml_dtypes.float8_e5m2, 14)}[fmt]
    v = np.moveaxis(np.asarray(x, np.float32).astype(ml_dtypes.bfloat16).astype(np.float64), axis, -1)
    blocks = v.reshape(v.shape[:-1] + (-1, 32))
    amax = np.abs(blocks).max(-1, keepdims=True)
    byte = np.maximum(np.where(amax > 0, np.frexp(amax)[1] - 1 + 127, 0) - down, 1)
    scale = np.exp2(byte - 127.0)
    codes = (blocks / scale).astype(np.float32).astype(dtype).astype(np.float64)
    return np.moveaxis((codes * scale).reshape(v.shape), -1, axis)


WIDE = False


def mx_kscale(k):
    if not WIDE:
        return np.ones(k)
    levels = np.array([10, -10, 5, -5, 0])
    if k % 512:
        return np.exp2(np.random.permutation(np.resize(levels, k // 32))).repeat(32)
    a = np.empty((k // 512, 16))
    for p in range(k // 512):
        a[p, :8] = np.random.permutation(np.resize(levels, 8))
        for g in range(8):
            far = levels[np.abs(levels - a[p, g]) >= 10]
            a[p, g + 8] = far[np.random.randint(len(far))]
    return np.exp2(a.ravel()).repeat(32)


def f64(x):
    return np.asarray(x).astype(np.float64)


def striped(idx):
    return np.tile(idx.reshape(-1, 16).T, (8, 1)).astype(np.uint16)


def unstriped(offs):
    return offs[:16].T.reshape(-1).astype(np.int64)


E2M1 = np.array([0.0, 0.5, 1.0, 1.5, 2.0, 3.0, 4.0, 6.0, -0.0, -0.5, -1.0, -1.5, -2.0, -3.0, -4.0, -6.0])


def pack_weight(w, fmt):
    k, n = w.shape
    w = f64(np.asarray(w, np.float32).astype(ml_dtypes.bfloat16)).reshape(k // 32, 32, n)
    amax = np.abs(w).max(1)
    if fmt == "e4m3":
        byte = np.frexp(amax)[1] - 1 + 127 - 7
    else:
        mant, ex = np.frexp(amax / 6.0)
        byte = np.where(mant > 0.5, ex, ex - 1) + 127
    byte = np.clip(np.where(amax > 0, byte, 1), 1, 254)
    scaled = (w * np.exp2(127.0 - byte)[:, None, :]).reshape(k, n).astype(np.float32)
    by_word = np.ascontiguousarray(scaled.reshape(k // 512, 128, 4, n).transpose(0, 1, 3, 2))
    if fmt == "e4m3":
        words = by_word.astype(ml_dtypes.float8_e4m3fn).view(np.uint8)
    else:
        c = by_word.astype(ml_dtypes.float4_e2m1fn).view(np.uint8) & 0xF
        words = (c[..., 0::2] | (c[..., 1::2] << 4)).reshape(k // 512, 128, 2 * n)
    return np.ascontiguousarray(words), np.ascontiguousarray(byte.astype(np.uint8).reshape(k // 512, 16, n))


def unpack_weight(words, scales, fmt):
    g, _, n = scales.shape
    words = np.ascontiguousarray(words).reshape(g, 128, n, -1)
    if fmt == "e4m3":
        vals = words.view(ml_dtypes.float8_e4m3fn).astype(np.float64)
    else:
        nib = np.empty((g, 128, n, 4), np.uint8)
        nib[..., 0::2] = words & 0xF
        nib[..., 1::2] = words >> 4
        vals = E2M1[nib]
    vals = vals * np.repeat(np.exp2(scales.astype(np.float64) - 127.0), 8, axis=1)[..., None]
    return vals.transpose(0, 1, 3, 2).reshape(g * 512, n)


def pack_table(v):
    words, scales = pack_weight(v, "e4m3")
    return np.concatenate([words.reshape(words.shape[0], -1), scales.reshape(scales.shape[0], -1)], axis=1)


def unpack_table(tab):
    g, t = tab.shape[0], tab.shape[1] // 528
    return unpack_weight(tab[:, :512 * t].reshape(g, 128, t, 4), tab[:, 512 * t:].reshape(g, 16, t), "e4m3")


def silu(v):
    return v / (1.0 + np.exp(-np.maximum(v, -700.0)))


K, M, T, S = 1536, 1024, 512, 256


def setup_inputs():
    n = np.random.standard_normal
    s = mx_kscale(K)[:, None]
    w = n((K, M)) / np.sqrt(K) / s
    p_w4 = pack_weight(w[512:], "e2m1")
    return {
        "tab": pack_table(n((K, T)) * s),
        "w8": (w[:512]).astype(np.float32),
        "w4_words": p_w4[0],
        "w4_scales": p_w4[1],
        "b": (0.3 * n(1024)).astype(np.float32),
        "wgo": np.tile(np.random.uniform(0.5, 2.0, S), (128, 1)).astype(np.float32),
        "offs": striped(np.random.permutation(T)[:S]),
        "offs2": striped(np.random.permutation(T)[:S]),
    }


def reference(tab, w8, w4_words, w4_scales, b, wgo, offs, offs2):
    tab_ = unpack_table(tab)[:, unstriped(offs)]
    w8_ = mxq(f64(w8), 0, "e4m3")
    w4_ = unpack_weight(w4_words, w4_scales, "e2m1")
    y = w8_.T @ tab_[:512] + w4_.T @ tab_[512:]
    out = np.zeros((M, T))
    out[:, unstriped(offs2)] = f64(wgo)[0] * (silu(y + f64(b)[:, None]))
    return out

@@ -1,0 +1,165 @@
+from contextlib import ExitStack
+
+import concourse.mybir as mybir
+from concourse.masks import make_identity
+
+K, M, T, S = 1536, 1024, 512, 256
+FLOPS = 2 * K * M * S
+
+F32 = mybir.dt.float32
+BF16 = mybir.dt.bfloat16
+I32 = mybir.dt.int32
+U32 = mybir.dt.uint32
+U16 = mybir.dt.uint16
+U8 = mybir.dt.uint8
+FP8X4 = mybir.dt.float8_e4m3fn_x4
+FP4X4 = mybir.dt.float4_e2m1fn_x4
+SILU = mybir.ActivationFunctionType.Silu
+MULT = mybir.AluOpType.mult
+
+P = 128
+PACK = 4
+PASSES = 3
+TILES = M // P
+HALF = S // 2
+PAGES = 4
+W4_SPLIT = 2
+TILES_PER_W4 = TILES // W4_SPLIT
+
+
+def tile_list_tabscat_o_silu_kernel(tc, tab, w8, w4_words, w4_scales, b, wgo, offs, offs2, out):
+    nc = tc.nc
+    with ExitStack() as ctx:
+        keep = ctx.enter_context(tc.tile_pool(name="keep", bufs=1))
+        psum = ctx.enter_context(tc.psum_pool(name="psum", bufs=1))
+
+        gather_list = keep.tile([P, S // 16], U16, name="gather_list")
+        scatter_list = keep.tile([P, S // 16], U16, name="scatter_list")
+        tab_words0 = keep.tile([P, T], I32, name="tab_words0", align_bytes=64)
+        tab_words12 = keep.tile([P, 2, T], I32, name="tab_words12", align_bytes=64)
+        tab_words = [tab_words0[:], tab_words12[:, 0, :], tab_words12[:, 1, :]]
+        tab_scales = keep.tile([P, PASSES, T], U8, name="tab_scales", align_bytes=64)
+        got_words = [keep.tile([P, S], I32, name=f"got_words{a}", align_bytes=64) for a in range(PASSES)]
+        got_scales = [keep.tile([P, S], U8, name=f"got_scales{a}", align_bytes=64) for a in range(PASSES)]
+        w4_codes = [keep.tile([P, 2, 2 * P * TILES_PER_W4], U8, name=f"w4_codes{h}", align_bytes=64) for h in range(W4_SPLIT)]
+        w4_planes = keep.tile([P, 2, M], U8, name="w4_planes", align_bytes=64)
+        w8_raw = [keep.tile([P, PACK, 2 * P], F32, name=f"w8_raw{d}", align_bytes=64) for d in range(TILES // 2)]
+        w8_grouped = [keep.tile([P, P, PACK], BF16, name=f"w8_grouped{c}", align_bytes=64) for c in range(TILES)]
+        w8_codes = [keep.tile([P, P], U32, name=f"w8_codes{c}", align_bytes=64) for c in range(TILES)]
+        w8_planes = [keep.tile([P, P], U8, name=f"w8_planes{c}", align_bytes=64) for c in range(TILES)]
+        weights = keep.tile([P, S], F32, name="weights")
+        pages = [keep.tile([P, T], F32, name=f"page{g}") for g in range(PAGES)]
+        bias_rows = keep.tile([P, P], F32, name="bias_rows")
+        identity = keep.tile([P, P], F32, name="identity")
+        bias = keep.tile([P, TILES], F32, name="bias")
+        warm = keep.tile([P, 8], F32, name="warm")
+        sums = [psum.tile([P, S], F32, name=f"sums{g}") for g in range(4)]
+        bias_psum = psum.tile([P, P], F32, name="bias_psum")
+
+        tab32 = tab.bitcast(I32)
+        tab_word_rows = tab32[:, 0 : P * T].rearrange("a (p t) -> p a t", p=P)
+        tab_scale_rows = tab32[:, P * T :].rearrange("a (q t) -> q a t", q=16)
+        w4_words32 = w4_words.bitcast(I32).rearrange("a p n -> p a n")
+        w4_scale_rows = w4_scales.bitcast(I32).rearrange("a q n -> q a n")
+        w8_rows = w8.rearrange("(p j) n -> p j n", j=PACK)
+
+        nc.vector.memset(tab_scales[:].bitcast(I32), 0)
+        nc.vector.memset(w4_planes[:].bitcast(I32), 0)
+        nc.gpsimd.memset(bias_rows[:], 0.0)
+        nc.scalar.activation(warm[:, 0:1], bias_rows[:, 0:1], SILU)
+        nc.gpsimd.dma_start(out=bias_rows[0:TILES, :], in_=b.rearrange("(c p) -> c p", p=P))
+        make_identity(nc, identity[:])
+        for page in pages:
+            nc.vector.memset(page[:].bitcast(I32), 0)
+
+        def load_w8(d):
+            nc.sync.dma_start(out=w8_raw[d][:], in_=w8_rows[:, :, 2 * d * P : 2 * (d + 1) * P])
+
+        def load_w4(h):
+            width = TILES_PER_W4 * P // 2
+            nc.sync.dma_start(out=w4_codes[h][:].bitcast(I32), in_=w4_words32[:, :, h * width : (h + 1) * width])
+
+        nc.sync.dma_start(gather_list[:], offs)
+        nc.sync.dma_start(out=tab_words0[:], in_=tab_word_rows[:, 0, :])
+        for q in range(4):
+            nc.sync.dma_start(out=tab_scales[32 * q : 32 * q + 4].bitcast(I32), in_=tab_scale_rows[4 * q : 4 * q + 4])
+        nc.sync.dma_start(out=tab_words12[:], in_=tab_word_rows[:, 1:3, :])
+        load_w8(0)
+        load_w4(0)
+        nc.sync.dma_start(scatter_list[:], offs2)
+        for q in range(4):
+            nc.sync.dma_start(out=w4_planes[32 * q : 32 * q + 4].bitcast(I32), in_=w4_scale_rows[4 * q : 4 * q + 4])
+        nc.sync.dma_start(out=weights[:], in_=wgo)
+        load_w8(1)
+        load_w8(2)
+        load_w4(1)
+        load_w8(3)
+
+        nc.tensor.transpose(bias_psum[:], bias_rows[:], identity[:])
+        nc.scalar.copy(bias[:], bias_psum[:, 0:TILES])
+
+        def gather(a):
+            nc.vector.tensor_copy(got_words[a][:].bitcast(U32), tab_words[a].bitcast(U32).indirect(gather_list[:]))
+            nc.vector.tensor_copy(got_scales[a][:], tab_scales[:, a, :].indirect(gather_list[:]))
+
+        def interleave(c):
+            nc.scalar.copy(
+                w8_grouped[c][:].rearrange("p (n i) j -> p n j i", i=4),
+                w8_raw[c // 2][:, :, (c % 2) * P : (c % 2 + 1) * P].rearrange("p j (n i) -> p n j i", i=4),
+            )
+
+        def quantize(c):
+            nc.vector.quantize_mx(
+                out=w8_codes[c][:].bitcast(FP8X4),
+                scales=w8_planes[c][:],
+                in_=w8_grouped[c][:].rearrange("p n j -> p (n j)"),
+            )
+
+        def activated(c):
+            return w8_raw[min(c + 1, TILES - 1) // 2][:, c % PACK, :]
+
+        def project(c):
+            acc = sums[c % 4]
+            h, r = divmod(c, TILES_PER_W4)
+            for u in range(2):
+                cols = slice(u * HALF, (u + 1) * HALF)
+                for a in (1, 2):
+                    nc.tensor.matmul_mx(
+                        out=acc[:, cols],
+                        lhsT=w4_codes[h][:, a - 1, 2 * P * r : 2 * P * (r + 1)].bitcast(FP4X4),
+                        lhsT_scale=w4_planes[:, a - 1, c * P : (c + 1) * P],
+                        rhs=got_words[a][:, cols].bitcast(FP8X4),
+                        rhs_scale=got_scales[a][:, cols],
+                        start=(a == 1),
+                        stop=False,
+                    )
+                nc.tensor.matmul_mx(
+                    out=acc[:, cols],
+                    lhsT=w8_codes[c][:].bitcast(FP8X4),
+                    lhsT_scale=w8_planes[c][:],
+                    rhs=got_words[0][:, cols].bitcast(FP8X4),
+                    rhs_scale=got_scales[0][:, cols],
+                    start=False,
+                    stop=True,
+                )
+            nc.scalar.activation(activated(c), acc[:], SILU, bias=bias[:, c : c + 1])
+
+        def place(c):
+            page = pages[c % PAGES]
+            nc.vector.tensor_tensor(page[:].indirect(scatter_list[:]), activated(c), weights[:], MULT)
+            nc.sync.dma_start(out=out[c * P : (c + 1) * P, :], in_=page[:])
+
+        gather(0)
+        gather(1)
+        interleave(0)
+        gather(2)
+        quantize(0)
+        interleave(1)
+        quantize(1)
+        for c in range(TILES):
+            if c % 2 == 1 and c + 1 < TILES:
+                for ahead in (c + 1, c + 2):
+                    interleave(ahead)
+                    quantize(ahead)
+            project(c)
+            place(c)

@@ -22,9 +22,8 @@ PACK = 4
 PASSES = 3
 TILES = M // P
 HALF = S // 2
-PAGES = 4
-W4_SPLIT = 2
-TILES_PER_W4 = TILES // W4_SPLIT
+PAGES = 3
+FIRST = 2
 
 
 def tile_list_tabscat_o_silu_kernel(tc, tab, w8, w4_words, w4_scales, b, wgo, offs, offs2, out):
@@ -41,9 +40,12 @@ def tile_list_tabscat_o_silu_kernel(tc, tab, w8, w4_words, w4_scales, b, wgo, of
         tab_scales = keep.tile([P, PASSES, T], U8, name="tab_scales", align_bytes=64)
         got_words = [keep.tile([P, S], I32, name=f"got_words{a}", align_bytes=64) for a in range(PASSES)]
         got_scales = [keep.tile([P, S], U8, name=f"got_scales{a}", align_bytes=64) for a in range(PASSES)]
-        w4_codes = [keep.tile([P, 2, 2 * P * TILES_PER_W4], U8, name=f"w4_codes{h}", align_bytes=64) for h in range(W4_SPLIT)]
+        w4_first = keep.tile([P, 2, 2 * P * FIRST], U8, name="w4_first", align_bytes=64)
+        w4_rest = keep.tile([P, 2, 2 * P * (TILES - FIRST)], U8, name="w4_rest", align_bytes=64)
         w4_planes = keep.tile([P, 2, M], U8, name="w4_planes", align_bytes=64)
-        w8_raw = [keep.tile([P, PACK, 2 * P], F32, name=f"w8_raw{d}", align_bytes=64) for d in range(TILES // 2)]
+        w8_first = keep.tile([P, PACK, FIRST * P], F32, name="w8_first", align_bytes=64)
+        w8_rest = [keep.tile([P, PACK, P], F32, name=f"w8_rest{c}", align_bytes=64) for c in range(FIRST, TILES)]
+        w8_raw = [w8_first[:, :, c * P : (c + 1) * P] for c in range(FIRST)] + [t[:] for t in w8_rest]
         w8_grouped = [keep.tile([P, P, PACK], BF16, name=f"w8_grouped{c}", align_bytes=64) for c in range(TILES)]
         w8_codes = [keep.tile([P, P], U32, name=f"w8_codes{c}", align_bytes=64) for c in range(TILES)]
         w8_planes = [keep.tile([P, P], U8, name=f"w8_planes{c}", align_bytes=64) for c in range(TILES)]
@@ -53,7 +55,8 @@ def tile_list_tabscat_o_silu_kernel(tc, tab, w8, w4_words, w4_scales, b, wgo, of
         identity = keep.tile([P, P], F32, name="identity")
         bias = keep.tile([P, TILES], F32, name="bias")
         warm = keep.tile([P, 8], F32, name="warm")
-        sums = [psum.tile([P, S], F32, name=f"sums{g}") for g in range(4)]
+        sums = [psum.tile([P, S], F32, name=f"sums{g}") for g in range(6)]
+        first_half = keep.tile([P, HALF], F32, name="first_half")
         bias_psum = psum.tile([P, P], F32, name="bias_psum")
 
         tab32 = tab.bitcast(I32)
@@ -67,45 +70,44 @@ def tile_list_tabscat_o_silu_kernel(tc, tab, w8, w4_words, w4_scales, b, wgo, of
         nc.vector.memset(w4_planes[:].bitcast(I32), 0)
         nc.gpsimd.memset(bias_rows[:], 0.0)
         nc.scalar.activation(warm[:, 0:1], bias_rows[:, 0:1], SILU)
-        nc.gpsimd.dma_start(out=bias_rows[0:TILES, :], in_=b.rearrange("(c p) -> c p", p=P))
         make_identity(nc, identity[:])
         for page in pages:
             nc.vector.memset(page[:].bitcast(I32), 0)
-
-        def load_w8(d):
-            nc.sync.dma_start(out=w8_raw[d][:], in_=w8_rows[:, :, 2 * d * P : 2 * (d + 1) * P])
-
-        def load_w4(h):
-            width = TILES_PER_W4 * P // 2
-            nc.sync.dma_start(out=w4_codes[h][:].bitcast(I32), in_=w4_words32[:, :, h * width : (h + 1) * width])
 
         nc.sync.dma_start(gather_list[:], offs)
         nc.sync.dma_start(out=tab_words0[:], in_=tab_word_rows[:, 0, :])
         for q in range(4):
             nc.sync.dma_start(out=tab_scales[32 * q : 32 * q + 4].bitcast(I32), in_=tab_scale_rows[4 * q : 4 * q + 4])
+        nc.sync.dma_start(out=w8_first[:], in_=w8_rows[:, :, 0 : FIRST * P])
         nc.sync.dma_start(out=tab_words12[:], in_=tab_word_rows[:, 1:3, :])
-        load_w8(0)
-        load_w4(0)
-        nc.sync.dma_start(scatter_list[:], offs2)
+        nc.sync.dma_start(out=w4_first[:].bitcast(I32), in_=w4_words32[:, :, 0 : FIRST * P // 2])
+        nc.sync.dma_start(out=bias_rows[0:TILES, :], in_=b.rearrange("(c p) -> c p", p=P))
         for q in range(4):
             nc.sync.dma_start(out=w4_planes[32 * q : 32 * q + 4].bitcast(I32), in_=w4_scale_rows[4 * q : 4 * q + 4])
         nc.sync.dma_start(out=weights[:], in_=wgo)
-        load_w8(1)
-        load_w8(2)
-        load_w4(1)
-        load_w8(3)
+        nc.sync.dma_start(scatter_list[:], offs2)
+        for c in range(FIRST, TILES):
+            nc.sync.dma_start(out=w8_raw[c], in_=w8_rows[:, :, c * P : (c + 1) * P])
+            if c == FIRST:
+                nc.sync.dma_start(out=w4_rest[:].bitcast(I32), in_=w4_words32[:, :, FIRST * P // 2 :])
 
         nc.tensor.transpose(bias_psum[:], bias_rows[:], identity[:])
         nc.scalar.copy(bias[:], bias_psum[:, 0:TILES])
 
-        def gather(a):
-            nc.vector.tensor_copy(got_words[a][:].bitcast(U32), tab_words[a].bitcast(U32).indirect(gather_list[:]))
-            nc.vector.tensor_copy(got_scales[a][:], tab_scales[:, a, :].indirect(gather_list[:]))
+        def entries(offsets, cols):
+            return offsets[:, cols.start // 16 : cols.stop // 16]
+
+        def gather_words(a, cols):
+            window = tab_words[a].bitcast(U32)
+            nc.vector.tensor_copy(got_words[a][:, cols].bitcast(U32), window.indirect(entries(gather_list, cols)))
+
+        def gather_scales(a, cols):
+            nc.vector.tensor_copy(got_scales[a][:, cols], tab_scales[:, a, :].indirect(entries(gather_list, cols)))
 
         def interleave(c):
             nc.scalar.copy(
                 w8_grouped[c][:].rearrange("p (n i) j -> p n j i", i=4),
-                w8_raw[c // 2][:, :, (c % 2) * P : (c % 2 + 1) * P].rearrange("p j (n i) -> p n j i", i=4),
+                w8_raw[c].rearrange("p j (n i) -> p n j i", i=4),
             )
 
         def quantize(c):
@@ -116,50 +118,67 @@ def tile_list_tabscat_o_silu_kernel(tc, tab, w8, w4_words, w4_scales, b, wgo, of
             )
 
         def activated(c):
-            return w8_raw[min(c + 1, TILES - 1) // 2][:, c % PACK, :]
+            if c == 0 or c == TILES - 1:
+                return w8_first[:, min(c, 1), :]
+            return w8_raw[c + 1].rearrange("p j n -> p (j n)")[:, 0:S]
 
-        def project(c):
-            acc = sums[c % 4]
-            h, r = divmod(c, TILES_PER_W4)
-            for u in range(2):
-                cols = slice(u * HALF, (u + 1) * HALF)
-                for a in (1, 2):
-                    nc.tensor.matmul_mx(
-                        out=acc[:, cols],
-                        lhsT=w4_codes[h][:, a - 1, 2 * P * r : 2 * P * (r + 1)].bitcast(FP4X4),
-                        lhsT_scale=w4_planes[:, a - 1, c * P : (c + 1) * P],
-                        rhs=got_words[a][:, cols].bitcast(FP8X4),
-                        rhs_scale=got_scales[a][:, cols],
-                        start=(a == 1),
-                        stop=False,
-                    )
+        def multiply(c, acc, cols):
+            w4_codes, r = (w4_first, c) if c < FIRST else (w4_rest, c - FIRST)
+            for a in (1, 0, 2):
+                if a == 0:
+                    codes = w8_codes[c][:].bitcast(FP8X4)
+                    plane = w8_planes[c][:]
+                else:
+                    codes = w4_codes[:, a - 1, 2 * P * r : 2 * P * (r + 1)].bitcast(FP4X4)
+                    plane = w4_planes[:, a - 1, c * P : (c + 1) * P]
                 nc.tensor.matmul_mx(
-                    out=acc[:, cols],
-                    lhsT=w8_codes[c][:].bitcast(FP8X4),
-                    lhsT_scale=w8_planes[c][:],
-                    rhs=got_words[0][:, cols].bitcast(FP8X4),
-                    rhs_scale=got_scales[0][:, cols],
-                    start=False,
-                    stop=True,
+                    out=acc,
+                    lhsT=codes,
+                    lhsT_scale=plane,
+                    rhs=got_words[a][:, cols].bitcast(FP8X4),
+                    rhs_scale=got_scales[a][:, cols],
+                    start=(a == 1),
+                    stop=(a == 2),
                 )
-            nc.scalar.activation(activated(c), acc[:], SILU, bias=bias[:, c : c + 1])
 
-        def place(c):
+        def activate(c, values, acc):
+            nc.scalar.activation(values, acc, SILU, bias=bias[:, c : c + 1])
+
+        def place(c, values, cols):
             page = pages[c % PAGES]
-            nc.vector.tensor_tensor(page[:].indirect(scatter_list[:]), activated(c), weights[:], MULT)
-            nc.sync.dma_start(out=out[c * P : (c + 1) * P, :], in_=page[:])
+            nc.vector.tensor_tensor(page[:].indirect(entries(scatter_list, cols)), values, weights[:, cols], MULT)
 
-        gather(0)
-        gather(1)
+        def store(c):
+            nc.sync.dma_start(out=out[c * P : (c + 1) * P, :], in_=pages[c % PAGES][:])
+
+        whole = slice(0, S)
+        halves = (slice(0, HALF), slice(HALF, S))
+        gather_words(0, whole)
+        gather_scales(0, whole)
+        gather_scales(1, whole)
+        gather_scales(2, halves[0])
         interleave(0)
-        gather(2)
         quantize(0)
+        gather_words(1, whole)
+        gather_words(2, halves[0])
+        multiply(0, sums[0][:, halves[0]], halves[0])
+        activate(0, first_half[:], sums[0][:, halves[0]])
+        gather_scales(2, halves[1])
+        gather_words(2, halves[1])
         interleave(1)
         quantize(1)
-        for c in range(TILES):
-            if c % 2 == 1 and c + 1 < TILES:
-                for ahead in (c + 1, c + 2):
-                    interleave(ahead)
-                    quantize(ahead)
-            project(c)
-            place(c)
+        place(0, first_half[:], halves[0])
+        multiply(0, sums[1][:, halves[1]], halves[1])
+        activate(0, activated(0)[:, halves[1]], sums[1][:, halves[1]])
+        place(0, activated(0)[:, halves[1]], halves[1])
+        store(0)
+        for c in range(1, TILES):
+            if c + 1 < TILES:
+                interleave(c + 1)
+                quantize(c + 1)
+            acc = sums[(c + 1) % 6]
+            for cols in halves:
+                multiply(c, acc[:, cols], cols)
+            activate(c, activated(c), acc[:])
+            place(c, activated(c), whole)
+            store(c)

from contextlib import ExitStack

import concourse.mybir as mybir
from concourse.masks import make_identity

K, M, T, S = 1536, 1024, 512, 256
FLOPS = 2 * K * M * S

F32 = mybir.dt.float32
BF16 = mybir.dt.bfloat16
I32 = mybir.dt.int32
U32 = mybir.dt.uint32
U16 = mybir.dt.uint16
U8 = mybir.dt.uint8
FP8X4 = mybir.dt.float8_e4m3fn_x4
FP4X4 = mybir.dt.float4_e2m1fn_x4
SILU = mybir.ActivationFunctionType.Silu
MULT = mybir.AluOpType.mult

P = 128
PACK = 4
PASSES = 3
TILES = M // P
HALF = S // 2
PAGES = 3
FIRST = 2


def tile_list_tabscat_o_silu_kernel(tc, tab, w8, w4_words, w4_scales, b, wgo, offs, offs2, out):
    nc = tc.nc
    with ExitStack() as ctx:
        keep = ctx.enter_context(tc.tile_pool(name="keep", bufs=1))
        psum = ctx.enter_context(tc.psum_pool(name="psum", bufs=1))

        gather_list = keep.tile([P, S // 16], U16, name="gather_list")
        scatter_list = keep.tile([P, S // 16], U16, name="scatter_list")
        tab_words0 = keep.tile([P, T], I32, name="tab_words0", align_bytes=64)
        tab_words12 = keep.tile([P, 2, T], I32, name="tab_words12", align_bytes=64)
        tab_words = [tab_words0[:], tab_words12[:, 0, :], tab_words12[:, 1, :]]
        tab_scales = keep.tile([P, PASSES, T], U8, name="tab_scales", align_bytes=64)
        got_words = [keep.tile([P, S], I32, name=f"got_words{a}", align_bytes=64) for a in range(PASSES)]
        got_scales = [keep.tile([P, S], U8, name=f"got_scales{a}", align_bytes=64) for a in range(PASSES)]
        w4_first = keep.tile([P, 2, 2 * P * FIRST], U8, name="w4_first", align_bytes=64)
        w4_rest = keep.tile([P, 2, 2 * P * (TILES - FIRST)], U8, name="w4_rest", align_bytes=64)
        w4_planes = keep.tile([P, 2, M], U8, name="w4_planes", align_bytes=64)
        w8_first = keep.tile([P, PACK, FIRST * P], F32, name="w8_first", align_bytes=64)
        w8_rest = [keep.tile([P, PACK, P], F32, name=f"w8_rest{c}", align_bytes=64) for c in range(FIRST, TILES)]
        w8_raw = [w8_first[:, :, c * P : (c + 1) * P] for c in range(FIRST)] + [t[:] for t in w8_rest]
        w8_grouped = [keep.tile([P, P, PACK], BF16, name=f"w8_grouped{c}", align_bytes=64) for c in range(TILES)]
        w8_codes = [keep.tile([P, P], U32, name=f"w8_codes{c}", align_bytes=64) for c in range(TILES)]
        w8_planes = [keep.tile([P, P], U8, name=f"w8_planes{c}", align_bytes=64) for c in range(TILES)]
        weights = keep.tile([P, S], F32, name="weights")
        pages = [keep.tile([P, T], F32, name=f"page{g}") for g in range(PAGES)]
        bias_rows = keep.tile([P, P], F32, name="bias_rows")
        identity = keep.tile([P, P], F32, name="identity")
        bias = keep.tile([P, TILES], F32, name="bias")
        warm = keep.tile([P, 8], F32, name="warm")
        sums = [psum.tile([P, S], F32, name=f"sums{g}") for g in range(6)]
        first_half = keep.tile([P, HALF], F32, name="first_half")
        bias_psum = psum.tile([P, P], F32, name="bias_psum")

        tab32 = tab.bitcast(I32)
        tab_word_rows = tab32[:, 0 : P * T].rearrange("a (p t) -> p a t", p=P)
        tab_scale_rows = tab32[:, P * T :].rearrange("a (q t) -> q a t", q=16)
        w4_words32 = w4_words.bitcast(I32).rearrange("a p n -> p a n")
        w4_scale_rows = w4_scales.bitcast(I32).rearrange("a q n -> q a n")
        w8_rows = w8.rearrange("(p j) n -> p j n", j=PACK)

        nc.vector.memset(tab_scales[:].bitcast(I32), 0)
        nc.vector.memset(w4_planes[:].bitcast(I32), 0)
        nc.gpsimd.memset(bias_rows[:], 0.0)
        nc.scalar.activation(warm[:, 0:1], bias_rows[:, 0:1], SILU)
        make_identity(nc, identity[:])
        for page in pages:
            nc.vector.memset(page[:].bitcast(I32), 0)

        nc.sync.dma_start(gather_list[:], offs)
        nc.sync.dma_start(out=tab_words0[:], in_=tab_word_rows[:, 0, :])
        for q in range(4):
            nc.sync.dma_start(out=tab_scales[32 * q : 32 * q + 4].bitcast(I32), in_=tab_scale_rows[4 * q : 4 * q + 4])
        nc.sync.dma_start(out=w8_first[:], in_=w8_rows[:, :, 0 : FIRST * P])
        nc.sync.dma_start(out=tab_words12[:], in_=tab_word_rows[:, 1:3, :])
        nc.sync.dma_start(out=w4_first[:].bitcast(I32), in_=w4_words32[:, :, 0 : FIRST * P // 2])
        nc.sync.dma_start(out=bias_rows[0:TILES, :], in_=b.rearrange("(c p) -> c p", p=P))
        for q in range(4):
            nc.sync.dma_start(out=w4_planes[32 * q : 32 * q + 4].bitcast(I32), in_=w4_scale_rows[4 * q : 4 * q + 4])
        nc.sync.dma_start(out=weights[:], in_=wgo)
        nc.sync.dma_start(scatter_list[:], offs2)
        for c in range(FIRST, TILES):
            nc.sync.dma_start(out=w8_raw[c], in_=w8_rows[:, :, c * P : (c + 1) * P])
            if c == FIRST:
                nc.sync.dma_start(out=w4_rest[:].bitcast(I32), in_=w4_words32[:, :, FIRST * P // 2 :])

        nc.tensor.transpose(bias_psum[:], bias_rows[:], identity[:])
        nc.scalar.copy(bias[:], bias_psum[:, 0:TILES])

        def entries(offsets, cols):
            return offsets[:, cols.start // 16 : cols.stop // 16]

        def gather_words(a, cols):
            window = tab_words[a].bitcast(U32)
            nc.vector.tensor_copy(got_words[a][:, cols].bitcast(U32), window.indirect(entries(gather_list, cols)))

        def gather_scales(a, cols):
            nc.vector.tensor_copy(got_scales[a][:, cols], tab_scales[:, a, :].indirect(entries(gather_list, cols)))

        def interleave(c):
            nc.scalar.copy(
                w8_grouped[c][:].rearrange("p (n i) j -> p n j i", i=4),
                w8_raw[c].rearrange("p j (n i) -> p n j i", i=4),
            )

        def quantize(c):
            nc.vector.quantize_mx(
                out=w8_codes[c][:].bitcast(FP8X4),
                scales=w8_planes[c][:],
                in_=w8_grouped[c][:].rearrange("p n j -> p (n j)"),
            )

        def activated(c):
            if c == 0 or c == TILES - 1:
                return w8_first[:, min(c, 1), :]
            return w8_raw[c + 1].rearrange("p j n -> p (j n)")[:, 0:S]

        def multiply(c, acc, cols):
            w4_codes, r = (w4_first, c) if c < FIRST else (w4_rest, c - FIRST)
            for a in (1, 0, 2):
                if a == 0:
                    codes = w8_codes[c][:].bitcast(FP8X4)
                    plane = w8_planes[c][:]
                else:
                    codes = w4_codes[:, a - 1, 2 * P * r : 2 * P * (r + 1)].bitcast(FP4X4)
                    plane = w4_planes[:, a - 1, c * P : (c + 1) * P]
                nc.tensor.matmul_mx(
                    out=acc,
                    lhsT=codes,
                    lhsT_scale=plane,
                    rhs=got_words[a][:, cols].bitcast(FP8X4),
                    rhs_scale=got_scales[a][:, cols],
                    start=(a == 1),
                    stop=(a == 2),
                )

        def activate(c, values, acc):
            nc.scalar.activation(values, acc, SILU, bias=bias[:, c : c + 1])

        def place(c, values, cols):
            page = pages[c % PAGES]
            nc.vector.tensor_tensor(page[:].indirect(entries(scatter_list, cols)), values, weights[:, cols], MULT)

        def store(c):
            nc.sync.dma_start(out=out[c * P : (c + 1) * P, :], in_=pages[c % PAGES][:])

        whole = slice(0, S)
        halves = (slice(0, HALF), slice(HALF, S))
        gather_words(0, whole)
        gather_scales(0, whole)
        gather_scales(1, whole)
        gather_scales(2, halves[0])
        interleave(0)
        quantize(0)
        gather_words(1, whole)
        gather_words(2, halves[0])
        multiply(0, sums[0][:, halves[0]], halves[0])
        activate(0, first_half[:], sums[0][:, halves[0]])
        gather_scales(2, halves[1])
        gather_words(2, halves[1])
        interleave(1)
        quantize(1)
        place(0, first_half[:], halves[0])
        multiply(0, sums[1][:, halves[1]], halves[1])
        activate(0, activated(0)[:, halves[1]], sums[1][:, halves[1]])
        place(0, activated(0)[:, halves[1]], halves[1])
        store(0)
        for c in range(1, TILES):
            if c + 1 < TILES:
                interleave(c + 1)
                quantize(c + 1)
            acc = sums[(c + 1) % 6]
            for cols in halves:
                multiply(c, acc[:, cols], cols)
            activate(c, activated(c), acc[:])
            place(c, activated(c), whole)
            store(c)
